import numpy as np, ml_dtypes
CORES = [12,28,60,100,156,228]
N = 6
TK = 512
COEF = [[2,-1,0,1,0,-1],[-1,2,-1,0,1,0],[0,-1,2,-1,0,1],[1,0,-1,2,-1,0],[0,1,0,-1,2,-1],[-1,0,1,0,-1,2]]
def setup_inputs(rng):
    return {"x": rng.standard_normal((N, 128, TK), dtype=np.float32).astype(ml_dtypes.bfloat16), "a": (rng.standard_normal((N, 128, 128), dtype=np.float32) / 11).astype(ml_dtypes.bfloat16)}
def setup_inputs_big(rng):
    d = setup_inputs(rng)
    for k in ("x", "a"): d[k] = (d[k].astype(np.float32) * 1024.0).astype(d[k].dtype)
    return d
def setup_inputs_small(rng):
    d = setup_inputs(rng)
    for k in ("x", "a"): d[k] = (d[k].astype(np.float32) * (1 / 1024.0)).astype(d[k].dtype)
    return d
def setup_inputs_apart(rng):
    d = setup_inputs(rng)
    f = (10.0 ** rng.permutation(np.linspace(-1.5, 1.5, N))).astype(np.float32).reshape(N, 1, 1)
    for k in ("x", "a"): d[k] = (d[k].astype(np.float32) * f).astype(d[k].dtype)
    return d
def reference(x, a):
    X, A = x.astype(np.float64), a.astype(np.float64)
    y = np.stack([A[r].T @ sum(COEF[r][j] * X[j] for j in range(N)) for r in range(N)])
    return {"y": y.astype(ml_dtypes.bfloat16)}

@@ -1,0 +1,133 @@
+from concourse.bass import DstId, RemoteDMATransfer
+from concourse.mybir import AluOpType
+
+N = 6
+K = 128
+TK = 512
+
+SCRATCH = {
+    "xd": ("dram", [K, TK], "bfloat16"),
+    "xs": ("sbuf", [K, TK], "bfloat16"),
+    "a_s": ("sbuf", [K, K], "bfloat16"),
+    "kc": ("sbuf", [K, N * K], "bfloat16"),
+    "aw": ("sbuf", [K, N * K], "bfloat16"),
+    "ys": ("sbuf", [K, TK], "bfloat16"),
+    "ps": ("psum", [K, TK], "float32"),
+}
+for _j in range(N):
+    SCRATCH["land%d" % _j] = ("sbuf", [K, TK], "bfloat16")
+
+SEMAPHORES = ["ldd", "ldx", "lda", "rel", "sent", "vk", "va", "mm", "cp", "st"] + ["arr%d" % _j for _j in range(N)]
+
+
+def _bits(mask):
+    return [b for b in range(mask.bit_length()) if (mask >> b) & 1]
+
+
+def _count(mask):
+    return len(_bits(mask))
+
+
+def _plan(T, topo):
+    coef, cores = T.tables["COEF"], T.cores
+    wants = [[r for r in range(N) if r != j and coef[r][j] != 0] for j in range(N)]
+    straight = [[r for r in wants[j] if topo.may_write(cores[j], cores[r])] for j in range(N)]
+    far = [[r for r in wants[j] if r not in straight[j]] for j in range(N)]
+    via = []
+    for j in range(N):
+        src = cores[j]
+        span = topo.CORES_PER_CHIP
+        chipmates = [c for c in range(max(0, src - span + 1), src + span)
+                     if c != src and topo.host(c) == topo.host(src) and topo.chip(c) == topo.chip(src)]
+        used, hops = [], []
+        for k, r in enumerate(far[j]):
+            able = [c for c in chipmates if c not in used and topo.may_write(c, cores[r])]
+            turn = (k + [s for s in range(N) if r in far[s]].index(j)) % 2
+            near = [c for c in able if topo.die(c) == topo.die(src)]
+            other = [c for c in able if topo.die(c) != topo.die(src)]
+            first, second = (near, other) if turn == 0 else (other, near)
+            c = (first + second)[0]
+            used.append(c)
+            hops.append((c, r))
+        via.append(hops)
+    return straight, via
+
+
+def _dst(topo, dst, src):
+    rid, pid = topo.addr(dst, src)
+    return DstId(rid=rid, pnc=pid)
+
+
+def rank_program(g, core, T, topo):
+    cores, coef, sem = T.cores, T.tables["COEF"], T.sem
+    straight, via = _plan(T, topo)
+    rank = T.rank_of(core)
+
+    if rank is None:
+        for j in range(N):
+            for c, r in via[j]:
+                if c != core:
+                    continue
+                hand = topo.mask(cores[j], core) & ~topo.mask(core, cores[r])
+                out = topo.mask(core, cores[r])
+                rid, pid = topo.addr(cores[r], core)
+                g.wait_ge(sem.rel, _count(hand))
+                g.remote_dma(out_ap=T["land%d" % j][:], in_ap=T.xd[:], remote_sem=sem["arr%d" % j], local_sem=sem.sent,
+                             pid=pid, routing_id=rid, dma_engine_mask=out)
+                g.wait_ge(sem.sent, _count(out))
+        return
+
+    r = rank
+    g.sync.dma_start(T.xd[:], T.x[:]).then_inc(sem.ldd, 16)
+    g.sync.dma_start(T.xs[:], T.x[:]).then_inc(sem.ldx, 16)
+    g.sync.dma_start(T.a_s[:], T.a[:]).then_inc(sem.lda, 16)
+
+    g.wait_ge(sem.ldd, 16)
+    sent = 0
+    if via[r]:
+        c0, r0 = via[r][0]
+        hand = topo.mask(core, c0) & ~topo.mask(c0, cores[r0])
+        g.remote_dma_fused([RemoteDMATransfer(dst_ids=[_dst(topo, c, core) for c, _ in via[r]], dma_engine_mask=hand,
+                                              remote_sem=sem.rel, src=T.xd[:], dsts=[T.xd[:] for _ in via[r]])],
+                           local_sem=sem.sent)
+        sent += _count(hand)
+    if straight[r]:
+        out = topo.mask(core, cores[straight[r][0]])
+        g.remote_dma_fused([RemoteDMATransfer(dst_ids=[_dst(topo, cores[d], core) for d in straight[r]],
+                                              dma_engine_mask=out, remote_sem=sem["arr%d" % r], src=T.xd[:],
+                                              dsts=[T["land%d" % r][:] for _ in straight[r]])],
+                           local_sem=sem.sent)
+        sent += _count(out)
+    g.wait_ge(sem.sent, sent)
+
+    mine = [j for j in range(N) if coef[r][j] != 0]
+    v = g.vector
+    for j in mine:
+        v.memset(T.kc[:, j * K:(j + 1) * K], float(coef[r][j])).then_inc(sem.vk, 1)
+    v.wait_ge(sem.vk, len(mine))
+    v.wait_ge(sem.lda, 16)
+    for j in mine:
+        v.tensor_tensor(T.aw[:, j * K:(j + 1) * K], T.a_s[:], T.kc[:, j * K:(j + 1) * K], AluOpType.mult).then_inc(sem.va, 1)
+
+    t = g.tensor
+    near = [j for j in mine if j != r and r in straight[j]]
+    farj = [j for j in mine if j != r and r not in straight[j]]
+    order = [r] + near + farj
+    t.wait_ge(sem.va, len(mine))
+    t.wait_ge(sem.ldx, 16)
+    last = None
+    for i, j in enumerate(order):
+        if j == r:
+            rhs = T.xs[:]
+        else:
+            sender = cores[j] if j in near else [c for c, d in via[j] if d == r][0]
+            t.wait_ge(sem["arr%d" % j], _count(topo.mask(sender, core)))
+            rhs = T["land%d" % j][:]
+        last = t.matmul(T.ps[:], T.aw[:, j * K:(j + 1) * K], rhs, i == 0, i == len(order) - 1)
+    last.then_inc(sem.mm, 1)
+
+    v.wait_ge(sem.mm, 1)
+    v.tensor_copy(T.ys[:], T.ps[:]).then_inc(sem.cp, 1)
+    g.sync.wait_ge(sem.cp, 1)
+    g.sync.dma_start(T.y[:], T.ys[:]).then_inc(sem.st, 16)
+    g.sync.wait_ge(sem.st, 16)

@@ -4,6 +4,9 @@ from concourse.mybir import AluOpType
 N = 6
 K = 128
 TK = 512
+NH = 2
+W = TK // NH
+HE = 4
 
 SCRATCH = {
     "xd": ("dram", [K, TK], "bfloat16"),
@@ -12,43 +15,67 @@ SCRATCH = {
     "kc": ("sbuf", [K, N * K], "bfloat16"),
     "aw": ("sbuf", [K, N * K], "bfloat16"),
     "ys": ("sbuf", [K, TK], "bfloat16"),
-    "ps": ("psum", [K, TK], "float32"),
 }
 for _j in range(N):
     SCRATCH["land%d" % _j] = ("sbuf", [K, TK], "bfloat16")
+for _h in range(NH):
+    SCRATCH["xd%d" % _h] = ("dram", [K, W], "bfloat16")
+    SCRATCH["ps%d" % _h] = ("psum", [K, TK], "float32")
 
-SEMAPHORES = ["ldd", "ldx", "lda", "rel", "sent", "vk", "va", "mm", "cp", "st"] + ["arr%d" % _j for _j in range(N)]
+SEMAPHORES = (["ldw", "ldx", "lda", "sent", "vk", "va"]
+              + ["arr%dh%d" % (_j, _h) for _j in range(N) for _h in range(NH)]
+              + [n + "%d" % _h for _h in range(NH) for n in ("ld", "rel", "mm", "cp", "st")])
 
 
 def _bits(mask):
     return [b for b in range(mask.bit_length()) if (mask >> b) & 1]
 
 
-def _count(mask):
-    return len(_bits(mask))
+def _group(mask, k, top):
+    b = _bits(mask)
+    if top:
+        b = b[::-1]
+    return sum(1 << e for e in b[k * HE:(k + 1) * HE])
 
 
 def _plan(T, topo):
     coef, cores = T.tables["COEF"], T.cores
     wants = [[r for r in range(N) if r != j and coef[r][j] != 0] for j in range(N)]
-    straight = [[r for r in wants[j] if topo.may_write(cores[j], cores[r])] for j in range(N)]
-    far = [[r for r in wants[j] if r not in straight[j]] for j in range(N)]
+    can = [[j for j in range(N) if r in wants[j] and topo.may_write(cores[j], cores[r])] for r in range(N)]
+    straight = [[r for r in wants[j] if j in can[r] and can[r].index(j) % 2 == 0][:1] for j in range(N)]
+    around = [[r for r in wants[j] if j in can[r] and r not in straight[j]] for j in range(N)]
+    cross = [[r for r in wants[j] if j not in can[r]] for j in range(N)]
+    xsrc = [[j for j in range(N) if r in cross[j]] for r in range(N)]
     via = []
     for j in range(N):
         src = cores[j]
         span = topo.CORES_PER_CHIP
         chipmates = [c for c in range(max(0, src - span + 1), src + span)
                      if c != src and topo.host(c) == topo.host(src) and topo.chip(c) == topo.chip(src)]
-        used, hops = [], []
-        for k, r in enumerate(far[j]):
+        used, hops, split = [], [], []
+
+        def take(r, turn):
             able = [c for c in chipmates if c not in used and topo.may_write(c, cores[r])]
-            turn = (k + [s for s in range(N) if r in far[s]].index(j)) % 2
             near = [c for c in able if topo.die(c) == topo.die(src)]
             other = [c for c in able if topo.die(c) != topo.die(src)]
-            first, second = (near, other) if turn == 0 else (other, near)
-            c = (first + second)[0]
+            c = (near + other if turn == 0 else other + near)[0]
             used.append(c)
-            hops.append((c, r))
+            return c
+
+        for k, r in enumerate(cross[j]):
+            n, i = len(xsrc[r]), xsrc[r].index(j)
+            odd = n % 2 == 1
+            split.append(odd and i == n // 2)
+            hops.append([take(r, (k + i - (1 if odd and i > n // 2 else 0)) % 2), [r, r]])
+        if len(hops) % 2 == 1:
+            split[-1] = False
+        for k, r in enumerate(around[j]):
+            split.append(len(xsrc[r]) % 2 == 0)
+            hops.append([take(r, (k + 1) % 2), [r, r]])
+        for k in range(len(hops) - 1):
+            if split[k] and split[k + 1]:
+                hops[k][1][1], hops[k + 1][1][1] = hops[k + 1][1][1], hops[k][1][1]
+                split[k] = split[k + 1] = False
         via.append(hops)
     return straight, via
 
@@ -62,42 +89,49 @@ def rank_program(g, core, T, topo):
     cores, coef, sem = T.cores, T.tables["COEF"], T.sem
     straight, via = _plan(T, topo)
     rank = T.rank_of(core)
+    late_first = list(range(NH))[::-1]
 
     if rank is None:
         for j in range(N):
-            for c, r in via[j]:
+            for c, to in via[j]:
                 if c != core:
                     continue
-                hand = topo.mask(cores[j], core) & ~topo.mask(core, cores[r])
-                out = topo.mask(core, cores[r])
-                rid, pid = topo.addr(cores[r], core)
-                g.wait_ge(sem.rel, _count(hand))
-                g.remote_dma(out_ap=T["land%d" % j][:], in_ap=T.xd[:], remote_sem=sem["arr%d" % j], local_sem=sem.sent,
-                             pid=pid, routing_id=rid, dma_engine_mask=out)
-                g.wait_ge(sem.sent, _count(out))
+                for n, h in enumerate(late_first):
+                    d = cores[to[h]]
+                    rid, pid = topo.addr(d, core)
+                    g.wait_ge(sem["rel%d" % h], HE)
+                    g.remote_dma(out_ap=T["land%d" % j][:, h * W:(h + 1) * W], in_ap=T["xd%d" % h][:],
+                                 remote_sem=sem["arr%dh%d" % (j, h)], local_sem=sem.sent, pid=pid, routing_id=rid,
+                                 dma_engine_mask=_group(topo.mask(core, d), n, False))
+                g.wait_ge(sem.sent, NH * HE)
         return
 
     r = rank
-    g.sync.dma_start(T.xd[:], T.x[:]).then_inc(sem.ldd, 16)
-    g.sync.dma_start(T.xs[:], T.x[:]).then_inc(sem.ldx, 16)
+    if via[r]:
+        g.sync.dma_start(T.xd0[:], T.x[:, 0:W]).then_inc(sem.ld0, 16)
+        g.scalar.dma_start(T.xd1[:], T.x[:, W:TK]).then_inc(sem.ld1, 16)
+    if straight[r]:
+        g.sync.dma_start(T.xd[:], T.x[:]).then_inc(sem.ldw, 16)
+    g.scalar.dma_start(T.xs[:], T.x[:]).then_inc(sem.ldx, 16)
     g.sync.dma_start(T.a_s[:], T.a[:]).then_inc(sem.lda, 16)
 
-    g.wait_ge(sem.ldd, 16)
     sent = 0
     if via[r]:
-        c0, r0 = via[r][0]
-        hand = topo.mask(core, c0) & ~topo.mask(c0, cores[r0])
-        g.remote_dma_fused([RemoteDMATransfer(dst_ids=[_dst(topo, c, core) for c, _ in via[r]], dma_engine_mask=hand,
-                                              remote_sem=sem.rel, src=T.xd[:], dsts=[T.xd[:] for _ in via[r]])],
-                           local_sem=sem.sent)
-        sent += _count(hand)
-    if straight[r]:
-        out = topo.mask(core, cores[straight[r][0]])
-        g.remote_dma_fused([RemoteDMATransfer(dst_ids=[_dst(topo, cores[d], core) for d in straight[r]],
-                                              dma_engine_mask=out, remote_sem=sem["arr%d" % r], src=T.xd[:],
-                                              dsts=[T["land%d" % r][:] for _ in straight[r]])],
-                           local_sem=sem.sent)
-        sent += _count(out)
+        for h in range(NH):
+            g.wait_ge(sem["ld%d" % h], 16)
+            g.remote_dma_fused([RemoteDMATransfer(dst_ids=[_dst(topo, c, core) for c, _ in via[r]],
+                                                  dma_engine_mask=_group(topo.mask(core, via[r][0][0]), h, True),
+                                                  remote_sem=sem["rel%d" % h], src=T["xd%d" % h][:],
+                                                  dsts=[T["xd%d" % h][:] for _ in via[r]])],
+                               local_sem=sem.sent)
+            sent += HE
+    for d in straight[r]:
+        out = topo.mask(core, cores[d])
+        rid, pid = topo.addr(cores[d], core)
+        g.wait_ge(sem.ldw, 16)
+        g.remote_dma(out_ap=T["land%d" % r][:], in_ap=T.xd[:], remote_sem=sem["arr%dh0" % r], local_sem=sem.sent,
+                     pid=pid, routing_id=rid, dma_engine_mask=out)
+        sent += len(_bits(out))
     g.wait_ge(sem.sent, sent)
 
     mine = [j for j in range(N) if coef[r][j] != 0]
@@ -113,21 +147,30 @@ def rank_program(g, core, T, topo):
     near = [j for j in mine if j != r and r in straight[j]]
     farj = [j for j in mine if j != r and r not in straight[j]]
     order = [r] + near + farj
+
+    def mm(j, h):
+        rhs = T.xs if j == r else T["land%d" % j]
+        i = t.matmul(T["ps%d" % h][:, 0:W], T.aw[:, j * K:(j + 1) * K], rhs[:, h * W:(h + 1) * W],
+                     j == order[0], j == order[-1])
+        if j == order[-1]:
+            i.then_inc(sem["mm%d" % h], 1)
+
     t.wait_ge(sem.va, len(mine))
     t.wait_ge(sem.ldx, 16)
-    last = None
-    for i, j in enumerate(order):
-        if j == r:
-            rhs = T.xs[:]
-        else:
-            sender = cores[j] if j in near else [c for c, d in via[j] if d == r][0]
-            t.wait_ge(sem["arr%d" % j], _count(topo.mask(sender, core)))
-            rhs = T["land%d" % j][:]
-        last = t.matmul(T.ps[:], T.aw[:, j * K:(j + 1) * K], rhs, i == 0, i == len(order) - 1)
-    last.then_inc(sem.mm, 1)
+    for j in [r] + near:
+        if j != r:
+            t.wait_ge(sem["arr%dh0" % j], len(_bits(topo.mask(cores[j], core))))
+        for h in late_first:
+            mm(j, h)
+    for h in late_first:
+        for j in farj:
+            t.wait_ge(sem["arr%dh%d" % (j, h)], HE)
+            mm(j, h)
 
-    v.wait_ge(sem.mm, 1)
-    v.tensor_copy(T.ys[:], T.ps[:]).then_inc(sem.cp, 1)
-    g.sync.wait_ge(sem.cp, 1)
-    g.sync.dma_start(T.y[:], T.ys[:]).then_inc(sem.st, 16)
-    g.sync.wait_ge(sem.st, 16)
+    for n, h in enumerate(late_first):
+        v.wait_ge(sem["mm%d" % h], 1)
+        v.tensor_copy(T.ys[:, h * W:(h + 1) * W], T["ps%d" % h][:, 0:W]).then_inc(sem["cp%d" % h], 1)
+        q = (g.scalar, g.sync)[n % 2]
+        q.wait_ge(sem["cp%d" % h], 1)
+        q.dma_start(T.y[:, h * W:(h + 1) * W], T.ys[:, h * W:(h + 1) * W]).then_inc(sem["st%d" % h], 16)
+        q.wait_ge(sem["st%d" % h], 16)

@@ -5,25 +5,31 @@ N = 6
 K = 128
 TK = 512
 NH = 2
-W = TK // NH
+WP = 16
+WB = (TK - WP) // NH
+COL = {"p": (0, WP), 0: (WP, WP + WB), 1: (WP + WB, TK)}
 HE = 4
 
 SCRATCH = {
     "xd": ("dram", [K, TK], "bfloat16"),
+    "xdp": ("dram", [K, WP], "bfloat16"),
     "xs": ("sbuf", [K, TK], "bfloat16"),
     "a_s": ("sbuf", [K, K], "bfloat16"),
     "kc": ("sbuf", [K, N * K], "bfloat16"),
     "aw": ("sbuf", [K, N * K], "bfloat16"),
     "ys": ("sbuf", [K, TK], "bfloat16"),
+    "psp": ("psum", [K, TK], "float32"),
 }
 for _j in range(N):
     SCRATCH["land%d" % _j] = ("sbuf", [K, TK], "bfloat16")
+    SCRATCH["lp%d" % _j] = ("dram", [K, WP], "bfloat16")
 for _h in range(NH):
-    SCRATCH["xd%d" % _h] = ("dram", [K, W], "bfloat16")
+    SCRATCH["xd%d" % _h] = ("dram", [K, WB], "bfloat16")
     SCRATCH["ps%d" % _h] = ("psum", [K, TK], "float32")
 
-SEMAPHORES = (["ldw", "ldx", "lda", "sent", "vk", "va"]
+SEMAPHORES = (["ldw", "ldx", "lda", "ldp", "relp", "mmp", "cpp", "sent", "vk", "va"]
               + ["arr%dh%d" % (_j, _h) for _j in range(N) for _h in range(NH)]
+              + [n + "%d" % _j for _j in range(N) for n in ("arrp", "lpd")]
               + [n + "%d" % _h for _h in range(NH) for n in ("ld", "rel", "mm", "cp", "st")])
 
 
@@ -31,11 +37,11 @@ def _bits(mask):
     return [b for b in range(mask.bit_length()) if (mask >> b) & 1]
 
 
-def _group(mask, k, top):
+def _group(mask, k, top, n=HE):
     b = _bits(mask)
     if top:
         b = b[::-1]
-    return sum(1 << e for e in b[k * HE:(k + 1) * HE])
+    return sum(1 << e for e in b[k * n:(k + 1) * n])
 
 
 def _plan(T, topo):
@@ -89,42 +95,46 @@ def rank_program(g, core, T, topo):
     cores, coef, sem = T.cores, T.tables["COEF"], T.sem
     straight, via = _plan(T, topo)
     rank = T.rank_of(core)
-    late_first = list(range(NH))[::-1]
 
     if rank is None:
         for j in range(N):
             for c, to in via[j]:
                 if c != core:
                     continue
-                for n, h in enumerate(late_first):
+                d = cores[to[0]]
+                rid, pid = topo.addr(d, core)
+                g.wait_ge(sem.relp, 1)
+                g.remote_dma(out_ap=T["lp%d" % j][:], in_ap=T.xdp[:], remote_sem=sem["arrp%d" % j], local_sem=sem.sent,
+                             pid=pid, routing_id=rid, dma_engine_mask=_group(topo.mask(core, d), 0, False, 1))
+                for h in range(NH):
                     d = cores[to[h]]
                     rid, pid = topo.addr(d, core)
                     g.wait_ge(sem["rel%d" % h], HE)
-                    g.remote_dma(out_ap=T["land%d" % j][:, h * W:(h + 1) * W], in_ap=T["xd%d" % h][:],
+                    g.remote_dma(out_ap=T["land%d" % j][:, COL[h][0]:COL[h][1]], in_ap=T["xd%d" % h][:],
                                  remote_sem=sem["arr%dh%d" % (j, h)], local_sem=sem.sent, pid=pid, routing_id=rid,
-                                 dma_engine_mask=_group(topo.mask(core, d), n, False))
-                g.wait_ge(sem.sent, NH * HE)
+                                 dma_engine_mask=_group(topo.mask(core, d), h, False))
+                g.wait_ge(sem.sent, 1 + NH * HE)
         return
 
     r = rank
-    if via[r]:
-        g.sync.dma_start(T.xd0[:], T.x[:, 0:W]).then_inc(sem.ld0, 16)
-        g.scalar.dma_start(T.xd1[:], T.x[:, W:TK]).then_inc(sem.ld1, 16)
+    g.sync.dma_start(T.xdp[:], T.x[:, COL["p"][0]:COL["p"][1]]).then_inc(sem.ldp, 16)
+    g.scalar.dma_start(T.xd0[:], T.x[:, COL[0][0]:COL[0][1]]).then_inc(sem.ld0, 16)
+    g.sync.dma_start(T.xd1[:], T.x[:, COL[1][0]:COL[1][1]]).then_inc(sem.ld1, 16)
     if straight[r]:
-        g.sync.dma_start(T.xd[:], T.x[:]).then_inc(sem.ldw, 16)
-    g.scalar.dma_start(T.xs[:], T.x[:]).then_inc(sem.ldx, 16)
+        g.scalar.dma_start(T.xd[:], T.x[:]).then_inc(sem.ldw, 16)
     g.sync.dma_start(T.a_s[:], T.a[:]).then_inc(sem.lda, 16)
+    g.scalar.dma_start(T.xs[:], T.x[:]).then_inc(sem.ldx, 16)
 
     sent = 0
-    if via[r]:
-        for h in range(NH):
-            g.wait_ge(sem["ld%d" % h], 16)
-            g.remote_dma_fused([RemoteDMATransfer(dst_ids=[_dst(topo, c, core) for c, _ in via[r]],
-                                                  dma_engine_mask=_group(topo.mask(core, via[r][0][0]), h, True),
-                                                  remote_sem=sem["rel%d" % h], src=T["xd%d" % h][:],
-                                                  dsts=[T["xd%d" % h][:] for _ in via[r]])],
-                               local_sem=sem.sent)
-            sent += HE
+    onchip = topo.mask(core, via[r][0][0])
+    for piece, buf, ld, rel, eng in ([("p", T.xdp, sem.ldp, sem.relp, _group(onchip, 0, True, 1))]
+                                     + [(h, T["xd%d" % h], sem["ld%d" % h], sem["rel%d" % h], _group(onchip, h, True))
+                                        for h in range(NH)]):
+        g.wait_ge(ld, 16)
+        g.remote_dma_fused([RemoteDMATransfer(dst_ids=[_dst(topo, c, core) for c, _ in via[r]], dma_engine_mask=eng,
+                                              remote_sem=rel, src=buf[:], dsts=[buf[:] for _ in via[r]])],
+                           local_sem=sem.sent)
+        sent += len(_bits(eng))
     for d in straight[r]:
         out = topo.mask(core, cores[d])
         rid, pid = topo.addr(cores[d], core)
@@ -135,6 +145,14 @@ def rank_program(g, core, T, topo):
     g.wait_ge(sem.sent, sent)
 
     mine = [j for j in range(N) if coef[r][j] != 0]
+    near = [j for j in mine if j != r and r in straight[j]]
+    farj = [j for j in mine if j != r and r not in straight[j]]
+    order = [r] + near + farj
+
+    for j in farj:
+        g.sync.wait_ge(sem["arrp%d" % j], 1)
+        g.sync.dma_start(T["land%d" % j][:, COL["p"][0]:COL["p"][1]], T["lp%d" % j][:]).then_inc(sem["lpd%d" % j], 16)
+
     v = g.vector
     for j in mine:
         v.memset(T.kc[:, j * K:(j + 1) * K], float(coef[r][j])).then_inc(sem.vk, 1)
@@ -144,33 +162,40 @@ def rank_program(g, core, T, topo):
         v.tensor_tensor(T.aw[:, j * K:(j + 1) * K], T.a_s[:], T.kc[:, j * K:(j + 1) * K], AluOpType.mult).then_inc(sem.va, 1)
 
     t = g.tensor
-    near = [j for j in mine if j != r and r in straight[j]]
-    farj = [j for j in mine if j != r and r not in straight[j]]
-    order = [r] + near + farj
+    bank = {"p": T.psp, 0: T.ps0, 1: T.ps1}
+    done = {"p": sem.mmp, 0: sem.mm0, 1: sem.mm1}
+    copied = {"p": sem.cpp, 0: sem.cp0, 1: sem.cp1}
+    pieces = [0, "p", 1]
 
-    def mm(j, h):
+    def mm(j, p):
         rhs = T.xs if j == r else T["land%d" % j]
-        i = t.matmul(T["ps%d" % h][:, 0:W], T.aw[:, j * K:(j + 1) * K], rhs[:, h * W:(h + 1) * W],
-                     j == order[0], j == order[-1])
+        lo, hi = COL[p]
+        i = t.matmul(bank[p][:, 0:hi - lo], T.aw[:, j * K:(j + 1) * K], rhs[:, lo:hi], j == order[0], j == order[-1])
         if j == order[-1]:
-            i.then_inc(sem["mm%d" % h], 1)
+            i.then_inc(done[p], 1)
 
     t.wait_ge(sem.va, len(mine))
     t.wait_ge(sem.ldx, 16)
     for j in [r] + near:
         if j != r:
             t.wait_ge(sem["arr%dh0" % j], len(_bits(topo.mask(cores[j], core))))
-        for h in late_first:
-            mm(j, h)
-    for h in late_first:
+        for p in pieces:
+            mm(j, p)
+    for p in pieces:
         for j in farj:
-            t.wait_ge(sem["arr%dh%d" % (j, h)], HE)
-            mm(j, h)
+            if p == "p":
+                t.wait_ge(sem["lpd%d" % j], 16)
+            else:
+                t.wait_ge(sem["arr%dh%d" % (j, p)], HE)
+            mm(j, p)
 
-    for n, h in enumerate(late_first):
-        v.wait_ge(sem["mm%d" % h], 1)
-        v.tensor_copy(T.ys[:, h * W:(h + 1) * W], T["ps%d" % h][:, 0:W]).then_inc(sem["cp%d" % h], 1)
-        q = (g.scalar, g.sync)[n % 2]
-        q.wait_ge(sem["cp%d" % h], 1)
-        q.dma_start(T.y[:, h * W:(h + 1) * W], T.ys[:, h * W:(h + 1) * W]).then_inc(sem["st%d" % h], 16)
-        q.wait_ge(sem["st%d" % h], 16)
+    for p in pieces:
+        lo, hi = COL[p]
+        v.wait_ge(done[p], 1)
+        v.tensor_copy(T.ys[:, lo:hi], bank[p][:, 0:hi - lo]).then_inc(copied[p], 1)
+    for n, (q, ps) in enumerate([(g.scalar, ["p", 0]), (g.sync, [1])]):
+        for p in ps:
+            q.wait_ge(copied[p], 1)
+        lo, hi = COL[ps[0]][0], COL[ps[-1]][1]
+        q.dma_start(T.y[:, lo:hi], T.ys[:, lo:hi]).then_inc(sem["st%d" % n], 16)
+        q.wait_ge(sem["st%d" % n], 16)

@@ -7,8 +7,8 @@ TK = 512
 NH = 2
 WP = 16
 WB = (TK - WP) // NH
-COL = {"p": (0, WP), 0: (WP, WP + WB), 1: (WP + WB, TK)}
-HE = 4
+COL = {0: (0, WB), 1: (WB, NH * WB), "p": (NH * WB, TK)}
+HE = 8
 
 SCRATCH = {
     "xd": ("dram", [K, TK], "bfloat16"),
@@ -32,58 +32,92 @@ SEMAPHORES = (["ldw", "ldx", "lda", "ldp", "relp", "mmp", "cpp", "sent", "vk", "
               + [n + "%d" % _j for _j in range(N) for n in ("arrp", "lpd")]
               + [n + "%d" % _h for _h in range(NH) for n in ("ld", "rel", "mm", "cp", "st")])
 
+_MEMO = {}
+
 
 def _bits(mask):
     return [b for b in range(mask.bit_length()) if (mask >> b) & 1]
 
 
-def _group(mask, k, top, n=HE):
+def _group(mask, top, n):
     b = _bits(mask)
     if top:
         b = b[::-1]
-    return sum(1 << e for e in b[k * n:(k + 1) * n])
+    return sum(1 << e for e in b[:n])
 
 
 def _plan(T, topo):
+    if "plan" in _MEMO:
+        return _MEMO["plan"]
     coef, cores = T.tables["COEF"], T.cores
+    world = range((max(topo.host(c) for c in cores) + 1) * topo.CORES_PER_HOST)
+    dies = sorted({topo.die(c) for c in world})
+
+    def place(c):
+        return (topo.host(c), topo.chip(c))
+
     wants = [[r for r in range(N) if r != j and coef[r][j] != 0] for j in range(N)]
     can = [[j for j in range(N) if r in wants[j] and topo.may_write(cores[j], cores[r])] for r in range(N)]
     straight = [[r for r in wants[j] if j in can[r] and can[r].index(j) % 2 == 0][:1] for j in range(N)]
-    around = [[r for r in wants[j] if j in can[r] and r not in straight[j]] for j in range(N)]
-    cross = [[r for r in wants[j] if j not in can[r]] for j in range(N)]
-    xsrc = [[j for j in range(N) if r in cross[j]] for r in range(N)]
-    via = []
-    for j in range(N):
-        src = cores[j]
-        span = topo.CORES_PER_CHIP
-        chipmates = [c for c in range(max(0, src - span + 1), src + span)
-                     if c != src and topo.host(c) == topo.host(src) and topo.chip(c) == topo.chip(src)]
-        used, hops, split = [], [], []
+    pairs = [(j, r) for j in range(N) for r in wants[j] if r not in straight[j]]
 
-        def take(r, turn):
-            able = [c for c in chipmates if c not in used and topo.may_write(c, cores[r])]
-            near = [c for c in able if topo.die(c) == topo.die(src)]
-            other = [c for c in able if topo.die(c) != topo.die(src)]
-            c = (near + other if turn == 0 else other + near)[0]
-            used.append(c)
-            return c
+    def able(j, r, kind, die):
+        s, d = cores[j], cores[r]
+        if kind == "near":
+            return [c for c in world if c != s and place(c) == place(s) and topo.die(c) == die and topo.may_write(c, d)]
+        return [c for c in world if topo.mates(c, d) and topo.die(c) == die and topo.may_write(c, d) and topo.may_write(s, c)]
 
-        for k, r in enumerate(cross[j]):
-            n, i = len(xsrc[r]), xsrc[r].index(j)
-            odd = n % 2 == 1
-            split.append(odd and i == n // 2)
-            hops.append([take(r, (k + i - (1 if odd and i > n // 2 else 0)) % 2), [r, r]])
-        if len(hops) % 2 == 1:
-            split[-1] = False
-        for k, r in enumerate(around[j]):
-            split.append(len(xsrc[r]) % 2 == 0)
-            hops.append([take(r, (k + 1) % 2), [r, r]])
-        for k in range(len(hops) - 1):
-            if split[k] and split[k + 1]:
-                hops[k][1][1], hops[k + 1][1][1] = hops[k + 1][1][1], hops[k][1][1]
-                split[k] = split[k + 1] = False
-        via.append(hops)
-    return straight, via
+    def links(j, r, kind, die):
+        s, d = cores[j], cores[r]
+        if kind == "straight":
+            return [("out", place(s), die), ("in", place(d), die), ("low", j)]
+        if kind == "near":
+            if topo.may_write(s, d):
+                return [("out", place(s), die), ("in", place(d), die), ("up", j)]
+            return [("mate", place(s), die), ("out", "mate of", place(s), die), ("in", place(d), die), ("up", j)]
+        return [("out", place(s), topo.die(s)), ("in", "mate of", place(d), topo.die(s)),
+                ("mate", "mate of", place(d), die), ("low", j)]
+
+    opts = {p: [(k, e) for k in ("near", "far") for e in dies
+                if able(p[0], p[1], k, e) and not (k == "far" and topo.may_write(cores[p[0]], cores[p[1]]))] for p in pairs}
+    weight = {"out": 0.75, "in": 1.0, "mate": 1.0, "low": 1.1, "up": 0.6}
+    early = 0.25
+
+    def score(way):
+        load = {}
+        for j in range(N):
+            for r in straight[j]:
+                for l in links(j, r, "straight", topo.die(cores[j])):
+                    load[l] = load.get(l, 0) + early * weight[l[0]]
+        for p, o in way.items():
+            for l in links(p[0], p[1], o[0], o[1]):
+                load[l] = load.get(l, 0) + weight[l[0]]
+        return sorted(load.values(), reverse=True)
+
+    way = {p: opts[p][0] for p in pairs}
+    best = score(way)
+    better = True
+    while better:
+        better = False
+        for p in pairs:
+            for q in pairs:
+                for o in opts[p]:
+                    for u in opts[q]:
+                        t = dict(way)
+                        t[q] = u
+                        t[p] = o
+                        s = score(t)
+                        if s < best:
+                            way, best, better = t, s, True
+    used, via = [], [[] for _ in range(N)]
+    for cross in (True, False):
+        for p in pairs:
+            if topo.may_write(cores[p[0]], cores[p[1]]) != cross:
+                c = [c for c in able(p[0], p[1], way[p][0], way[p][1]) if c not in used and c not in cores][-1 if cross else 0]
+                used.append(c)
+                via[p[0]].append([c, p[1]])
+    _MEMO["plan"] = (straight, via)
+    return _MEMO["plan"]
 
 
 def _dst(topo, dst, src):
@@ -101,18 +135,16 @@ def rank_program(g, core, T, topo):
             for c, to in via[j]:
                 if c != core:
                     continue
-                d = cores[to[0]]
+                d = cores[to]
                 rid, pid = topo.addr(d, core)
                 g.wait_ge(sem.relp, 1)
                 g.remote_dma(out_ap=T["lp%d" % j][:], in_ap=T.xdp[:], remote_sem=sem["arrp%d" % j], local_sem=sem.sent,
-                             pid=pid, routing_id=rid, dma_engine_mask=_group(topo.mask(core, d), 0, False, 1))
+                             pid=pid, routing_id=rid, dma_engine_mask=_group(topo.mask(core, d), False, 1))
                 for h in range(NH):
-                    d = cores[to[h]]
-                    rid, pid = topo.addr(d, core)
                     g.wait_ge(sem["rel%d" % h], HE)
                     g.remote_dma(out_ap=T["land%d" % j][:, COL[h][0]:COL[h][1]], in_ap=T["xd%d" % h][:],
                                  remote_sem=sem["arr%dh%d" % (j, h)], local_sem=sem.sent, pid=pid, routing_id=rid,
-                                 dma_engine_mask=_group(topo.mask(core, d), h, False))
+                                 dma_engine_mask=_group(topo.mask(core, d), False, HE))
                 g.wait_ge(sem.sent, 1 + NH * HE)
         return
 
@@ -126,15 +158,20 @@ def rank_program(g, core, T, topo):
     g.scalar.dma_start(T.xs[:], T.x[:]).then_inc(sem.ldx, 16)
 
     sent = 0
-    onchip = topo.mask(core, via[r][0][0])
-    for piece, buf, ld, rel, eng in ([("p", T.xdp, sem.ldp, sem.relp, _group(onchip, 0, True, 1))]
-                                     + [(h, T["xd%d" % h], sem["ld%d" % h], sem["rel%d" % h], _group(onchip, h, True))
-                                        for h in range(NH)]):
+    wide = max(topo.mask(core, c) for c, _ in via[r])
+    nearh = [c for c, _ in via[r] if topo.mask(core, c) == wide]
+    farh = [c for c, _ in via[r] if topo.mask(core, c) != wide]
+    for buf, ld, rel, n in ([(T.xdp, sem.ldp, sem.relp, 1)]
+                            + [(T["xd%d" % h], sem["ld%d" % h], sem["rel%d" % h], HE) for h in range(NH)]):
         g.wait_ge(ld, 16)
-        g.remote_dma_fused([RemoteDMATransfer(dst_ids=[_dst(topo, c, core) for c, _ in via[r]], dma_engine_mask=eng,
-                                              remote_sem=rel, src=buf[:], dsts=[buf[:] for _ in via[r]])],
-                           local_sem=sem.sent)
-        sent += len(_bits(eng))
+        trs = []
+        for hs, top in ((nearh, True), (farh, False)):
+            if hs:
+                trs.append(RemoteDMATransfer(dst_ids=[_dst(topo, c, core) for c in hs],
+                                             dma_engine_mask=_group(topo.mask(core, hs[0]), top, n),
+                                             remote_sem=rel, src=buf[:], dsts=[buf[:] for _ in hs]))
+                sent += n
+        g.remote_dma_fused(trs, local_sem=sem.sent)
     for d in straight[r]:
         out = topo.mask(core, cores[d])
         rid, pid = topo.addr(cores[d], core)
@@ -165,7 +202,7 @@ def rank_program(g, core, T, topo):
     bank = {"p": T.psp, 0: T.ps0, 1: T.ps1}
     done = {"p": sem.mmp, 0: sem.mm0, 1: sem.mm1}
     copied = {"p": sem.cpp, 0: sem.cp0, 1: sem.cp1}
-    pieces = [0, "p", 1]
+    pieces = [0, 1, "p"]
 
     def mm(j, p):
         rhs = T.xs if j == r else T["land%d" % j]
@@ -193,7 +230,7 @@ def rank_program(g, core, T, topo):
         lo, hi = COL[p]
         v.wait_ge(done[p], 1)
         v.tensor_copy(T.ys[:, lo:hi], bank[p][:, 0:hi - lo]).then_inc(copied[p], 1)
-    for n, (q, ps) in enumerate([(g.scalar, ["p", 0]), (g.sync, [1])]):
+    for n, (q, ps) in enumerate([(g.scalar, [0]), (g.sync, [1, "p"])]):
         for p in ps:
             q.wait_ge(copied[p], 1)
         lo, hi = COL[ps[0]][0], COL[ps[-1]][1]

from concourse.bass import DstId, RemoteDMATransfer
from concourse.mybir import AluOpType

N = 6
K = 128
TK = 512
NH = 2
WP = 16
WB = (TK - WP) // NH
COL = {0: (0, WB), 1: (WB, NH * WB), "p": (NH * WB, TK)}
HE = 8

SCRATCH = {
    "xd": ("dram", [K, TK], "bfloat16"),
    "xdp": ("dram", [K, WP], "bfloat16"),
    "xs": ("sbuf", [K, TK], "bfloat16"),
    "a_s": ("sbuf", [K, K], "bfloat16"),
    "kc": ("sbuf", [K, N * K], "bfloat16"),
    "aw": ("sbuf", [K, N * K], "bfloat16"),
    "ys": ("sbuf", [K, TK], "bfloat16"),
    "psp": ("psum", [K, TK], "float32"),
}
for _j in range(N):
    SCRATCH["land%d" % _j] = ("sbuf", [K, TK], "bfloat16")
    SCRATCH["lp%d" % _j] = ("dram", [K, WP], "bfloat16")
for _h in range(NH):
    SCRATCH["xd%d" % _h] = ("dram", [K, WB], "bfloat16")
    SCRATCH["ps%d" % _h] = ("psum", [K, TK], "float32")

SEMAPHORES = (["ldw", "ldx", "lda", "ldp", "relp", "mmp", "cpp", "sent", "vk", "va"]
              + ["arr%dh%d" % (_j, _h) for _j in range(N) for _h in range(NH)]
              + [n + "%d" % _j for _j in range(N) for n in ("arrp", "lpd")]
              + [n + "%d" % _h for _h in range(NH) for n in ("ld", "rel", "mm", "cp", "st")])

_MEMO = {}


def _bits(mask):
    return [b for b in range(mask.bit_length()) if (mask >> b) & 1]


def _group(mask, top, n):
    b = _bits(mask)
    if top:
        b = b[::-1]
    return sum(1 << e for e in b[:n])


def _plan(T, topo):
    if "plan" in _MEMO:
        return _MEMO["plan"]
    coef, cores = T.tables["COEF"], T.cores
    world = range((max(topo.host(c) for c in cores) + 1) * topo.CORES_PER_HOST)
    dies = sorted({topo.die(c) for c in world})

    def place(c):
        return (topo.host(c), topo.chip(c))

    wants = [[r for r in range(N) if r != j and coef[r][j] != 0] for j in range(N)]
    can = [[j for j in range(N) if r in wants[j] and topo.may_write(cores[j], cores[r])] for r in range(N)]
    straight = [[r for r in wants[j] if j in can[r] and can[r].index(j) % 2 == 0][:1] for j in range(N)]
    pairs = [(j, r) for j in range(N) for r in wants[j] if r not in straight[j]]

    def able(j, r, kind, die):
        s, d = cores[j], cores[r]
        if kind == "near":
            return [c for c in world if c != s and place(c) == place(s) and topo.die(c) == die and topo.may_write(c, d)]
        return [c for c in world if topo.mates(c, d) and topo.die(c) == die and topo.may_write(c, d) and topo.may_write(s, c)]

    def links(j, r, kind, die):
        s, d = cores[j], cores[r]
        if kind == "straight":
            return [("out", place(s), die), ("in", place(d), die), ("low", j)]
        if kind == "near":
            if topo.may_write(s, d):
                return [("out", place(s), die), ("in", place(d), die), ("up", j)]
            return [("mate", place(s), die), ("out", "mate of", place(s), die), ("in", place(d), die), ("up", j)]
        return [("out", place(s), topo.die(s)), ("in", "mate of", place(d), topo.die(s)),
                ("mate", "mate of", place(d), die), ("low", j)]

    opts = {p: [(k, e) for k in ("near", "far") for e in dies
                if able(p[0], p[1], k, e) and not (k == "far" and topo.may_write(cores[p[0]], cores[p[1]]))] for p in pairs}
    weight = {"out": 0.75, "in": 1.0, "mate": 1.0, "low": 1.1, "up": 0.6}
    early = 0.25

    def score(way):
        load = {}
        for j in range(N):
            for r in straight[j]:
                for l in links(j, r, "straight", topo.die(cores[j])):
                    load[l] = load.get(l, 0) + early * weight[l[0]]
        for p, o in way.items():
            for l in links(p[0], p[1], o[0], o[1]):
                load[l] = load.get(l, 0) + weight[l[0]]
        return sorted(load.values(), reverse=True)

    way = {p: opts[p][0] for p in pairs}
    best = score(way)
    better = True
    while better:
        better = False
        for p in pairs:
            for q in pairs:
                for o in opts[p]:
                    for u in opts[q]:
                        t = dict(way)
                        t[q] = u
                        t[p] = o
                        s = score(t)
                        if s < best:
                            way, best, better = t, s, True
    used, via = [], [[] for _ in range(N)]
    for cross in (True, False):
        for p in pairs:
            if topo.may_write(cores[p[0]], cores[p[1]]) != cross:
                c = [c for c in able(p[0], p[1], way[p][0], way[p][1]) if c not in used and c not in cores][-1 if cross else 0]
                used.append(c)
                via[p[0]].append([c, p[1]])
    _MEMO["plan"] = (straight, via)
    return _MEMO["plan"]


def _dst(topo, dst, src):
    rid, pid = topo.addr(dst, src)
    return DstId(rid=rid, pnc=pid)


def rank_program(g, core, T, topo):
    cores, coef, sem = T.cores, T.tables["COEF"], T.sem
    straight, via = _plan(T, topo)
    rank = T.rank_of(core)

    if rank is None:
        for j in range(N):
            for c, to in via[j]:
                if c != core:
                    continue
                d = cores[to]
                rid, pid = topo.addr(d, core)
                g.wait_ge(sem.relp, 1)
                g.remote_dma(out_ap=T["lp%d" % j][:], in_ap=T.xdp[:], remote_sem=sem["arrp%d" % j], local_sem=sem.sent,
                             pid=pid, routing_id=rid, dma_engine_mask=_group(topo.mask(core, d), False, 1))
                for h in range(NH):
                    g.wait_ge(sem["rel%d" % h], HE)
                    g.remote_dma(out_ap=T["land%d" % j][:, COL[h][0]:COL[h][1]], in_ap=T["xd%d" % h][:],
                                 remote_sem=sem["arr%dh%d" % (j, h)], local_sem=sem.sent, pid=pid, routing_id=rid,
                                 dma_engine_mask=_group(topo.mask(core, d), False, HE))
                g.wait_ge(sem.sent, 1 + NH * HE)
        return

    r = rank
    g.sync.dma_start(T.xdp[:], T.x[:, COL["p"][0]:COL["p"][1]]).then_inc(sem.ldp, 16)
    g.scalar.dma_start(T.xd0[:], T.x[:, COL[0][0]:COL[0][1]]).then_inc(sem.ld0, 16)
    g.sync.dma_start(T.xd1[:], T.x[:, COL[1][0]:COL[1][1]]).then_inc(sem.ld1, 16)
    if straight[r]:
        g.scalar.dma_start(T.xd[:], T.x[:]).then_inc(sem.ldw, 16)
    g.sync.dma_start(T.a_s[:], T.a[:]).then_inc(sem.lda, 16)
    g.scalar.dma_start(T.xs[:], T.x[:]).then_inc(sem.ldx, 16)

    sent = 0
    wide = max(topo.mask(core, c) for c, _ in via[r])
    nearh = [c for c, _ in via[r] if topo.mask(core, c) == wide]
    farh = [c for c, _ in via[r] if topo.mask(core, c) != wide]
    for buf, ld, rel, n in ([(T.xdp, sem.ldp, sem.relp, 1)]
                            + [(T["xd%d" % h], sem["ld%d" % h], sem["rel%d" % h], HE) for h in range(NH)]):
        g.wait_ge(ld, 16)
        trs = []
        for hs, top in ((nearh, True), (farh, False)):
            if hs:
                trs.append(RemoteDMATransfer(dst_ids=[_dst(topo, c, core) for c in hs],
                                             dma_engine_mask=_group(topo.mask(core, hs[0]), top, n),
                                             remote_sem=rel, src=buf[:], dsts=[buf[:] for _ in hs]))
                sent += n
        g.remote_dma_fused(trs, local_sem=sem.sent)
    for d in straight[r]:
        out = topo.mask(core, cores[d])
        rid, pid = topo.addr(cores[d], core)
        g.wait_ge(sem.ldw, 16)
        g.remote_dma(out_ap=T["land%d" % r][:], in_ap=T.xd[:], remote_sem=sem["arr%dh0" % r], local_sem=sem.sent,
                     pid=pid, routing_id=rid, dma_engine_mask=out)
        sent += len(_bits(out))
    g.wait_ge(sem.sent, sent)

    mine = [j for j in range(N) if coef[r][j] != 0]
    near = [j for j in mine if j != r and r in straight[j]]
    farj = [j for j in mine if j != r and r not in straight[j]]
    order = [r] + near + farj

    for j in farj:
        g.sync.wait_ge(sem["arrp%d" % j], 1)
        g.sync.dma_start(T["land%d" % j][:, COL["p"][0]:COL["p"][1]], T["lp%d" % j][:]).then_inc(sem["lpd%d" % j], 16)

    v = g.vector
    for j in mine:
        v.memset(T.kc[:, j * K:(j + 1) * K], float(coef[r][j])).then_inc(sem.vk, 1)
    v.wait_ge(sem.vk, len(mine))
    v.wait_ge(sem.lda, 16)
    for j in mine:
        v.tensor_tensor(T.aw[:, j * K:(j + 1) * K], T.a_s[:], T.kc[:, j * K:(j + 1) * K], AluOpType.mult).then_inc(sem.va, 1)

    t = g.tensor
    bank = {"p": T.psp, 0: T.ps0, 1: T.ps1}
    done = {"p": sem.mmp, 0: sem.mm0, 1: sem.mm1}
    copied = {"p": sem.cpp, 0: sem.cp0, 1: sem.cp1}
    pieces = [0, 1, "p"]

    def mm(j, p):
        rhs = T.xs if j == r else T["land%d" % j]
        lo, hi = COL[p]
        i = t.matmul(bank[p][:, 0:hi - lo], T.aw[:, j * K:(j + 1) * K], rhs[:, lo:hi], j == order[0], j == order[-1])
        if j == order[-1]:
            i.then_inc(done[p], 1)

    t.wait_ge(sem.va, len(mine))
    t.wait_ge(sem.ldx, 16)
    for j in [r] + near:
        if j != r:
            t.wait_ge(sem["arr%dh0" % j], len(_bits(topo.mask(cores[j], core))))
        for p in pieces:
            mm(j, p)
    for p in pieces:
        for j in farj:
            if p == "p":
                t.wait_ge(sem["lpd%d" % j], 16)
            else:
                t.wait_ge(sem["arr%dh%d" % (j, p)], HE)
            mm(j, p)

    for p in pieces:
        lo, hi = COL[p]
        v.wait_ge(done[p], 1)
        v.tensor_copy(T.ys[:, lo:hi], bank[p][:, 0:hi - lo]).then_inc(copied[p], 1)
    for n, (q, ps) in enumerate([(g.scalar, [0]), (g.sync, [1, "p"])]):
        for p in ps:
            q.wait_ge(copied[p], 1)
        lo, hi = COL[ps[0]][0], COL[ps[-1]][1]
        q.dma_start(T.y[:, lo:hi], T.ys[:, lo:hi]).then_inc(sem["st%d" % n], 16)
        q.wait_ge(sem["st%d" % n], 16)
